import numpy as np
import ml_dtypes


def mxq(x, axis, fmt="e4m3"):
    dtype, down = {"e4m3": (ml_dtypes.float8_e4m3fn, 7), "e5m2": (ml_dtypes.float8_e5m2, 14)}[fmt]
    v = np.moveaxis(np.asarray(x, np.float32).astype(ml_dtypes.bfloat16).astype(np.float64), axis, -1)
    blocks = v.reshape(v.shape[:-1] + (-1, 32))
    amax = np.abs(blocks).max(-1, keepdims=True)
    byte = np.maximum(np.where(amax > 0, np.frexp(amax)[1] - 1 + 127, 0) - down, 1)
    scale = np.exp2(byte - 127.0)
    codes = (blocks / scale).astype(np.float32).astype(dtype).astype(np.float64)
    return np.moveaxis((codes * scale).reshape(v.shape), -1, axis)


WIDE = False


def mx_kscale(k):
    if not WIDE:
        return np.ones(k)
    levels = np.array([10, -10, 5, -5, 0])
    if k % 512:
        return np.exp2(np.random.permutation(np.resize(levels, k // 32))).repeat(32)
    a = np.empty((k // 512, 16))
    for p in range(k // 512):
        a[p, :8] = np.random.permutation(np.resize(levels, 8))
        for g in range(8):
            far = levels[np.abs(levels - a[p, g]) >= 10]
            a[p, g + 8] = far[np.random.randint(len(far))]
    return np.exp2(a.ravel()).repeat(32)


def f64(x):
    return np.asarray(x).astype(np.float64)


def striped(idx):
    return np.tile(idx.reshape(-1, 16).T, (8, 1)).astype(np.uint16)


def unstriped(offs):
    return offs[:16].T.reshape(-1).astype(np.int64)


E2M1 = np.array([0.0, 0.5, 1.0, 1.5, 2.0, 3.0, 4.0, 6.0, -0.0, -0.5, -1.0, -1.5, -2.0, -3.0, -4.0, -6.0])


def pack_weight(w, fmt):
    k, n = w.shape
    w = f64(np.asarray(w, np.float32).astype(ml_dtypes.bfloat16)).reshape(k // 32, 32, n)
    amax = np.abs(w).max(1)
    if fmt == "e4m3":
        byte = np.frexp(amax)[1] - 1 + 127 - 7
    else:
        mant, ex = np.frexp(amax / 6.0)
        byte = np.where(mant > 0.5, ex, ex - 1) + 127
    byte = np.clip(np.where(amax > 0, byte, 1), 1, 254)
    scaled = (w * np.exp2(127.0 - byte)[:, None, :]).reshape(k, n).astype(np.float32)
    by_word = np.ascontiguousarray(scaled.reshape(k // 512, 128, 4, n).transpose(0, 1, 3, 2))
    if fmt == "e4m3":
        words = by_word.astype(ml_dtypes.float8_e4m3fn).view(np.uint8)
    else:
        c = by_word.astype(ml_dtypes.float4_e2m1fn).view(np.uint8) & 0xF
        words = (c[..., 0::2] | (c[..., 1::2] << 4)).reshape(k // 512, 128, 2 * n)
    return np.ascontiguousarray(words), np.ascontiguousarray(byte.astype(np.uint8).reshape(k // 512, 16, n))


def unpack_weight(words, scales, fmt):
    g, _, n = scales.shape
    words = np.ascontiguousarray(words).reshape(g, 128, n, -1)
    if fmt == "e4m3":
        vals = words.view(ml_dtypes.float8_e4m3fn).astype(np.float64)
    else:
        nib = np.empty((g, 128, n, 4), np.uint8)
        nib[..., 0::2] = words & 0xF
        nib[..., 1::2] = words >> 4
        vals = E2M1[nib]
    vals = vals * np.repeat(np.exp2(scales.astype(np.float64) - 127.0), 8, axis=1)[..., None]
    return vals.transpose(0, 1, 3, 2).reshape(g * 512, n)


def gelu(v):
    return 0.5 * v * (1.0 + np.tanh(np.sqrt(2.0 / np.pi) * (v + 0.044715 * v**3)))


K, H, T, S, T3, S2, P = 1024, 512, 4096, 1024, 2048, 1024, 512

def setup_inputs():
    n = np.random.standard_normal
    s = mx_kscale(K)[:, None]
    u = mx_kscale(H)[:, None]
    tab_words, tab_scales = pack_weight(n((K, T)) * s, "e4m3")
    tab2_words, tab2_scales = pack_weight(n((H, T3)) / np.sqrt(H) / u, "e4m3")
    w4_words, w4_scales = pack_weight(n((K, H)) / np.sqrt(K) / s, "e2m1")
    return {
        "tab_words": tab_words, "tab_scales": tab_scales,
        "tab2_words": tab2_words, "tab2_scales": tab2_scales,
        "offs": striped(np.random.permutation(T)[:S]),
        "offs2": striped(np.random.permutation(T3)[:S2]),
        "pos1": striped(np.random.permutation(S)[:P]),
        "pos2": striped(np.random.permutation(S)[:P]),
        "w1": (n((K, H)) / np.sqrt(K) / s).astype(np.float32),
        "w4_words": w4_words, "w4_scales": w4_scales,
        "shade": n((H, S)).astype(np.float32),
        "gain": (np.exp(0.4 * n(H)) * u[:, 0]).astype(np.float32),
        "seamw": n(S2).astype(np.float32),
        "level": (0.8 * n(S2)).astype(np.float32),
    }

def reference(tab_words, tab_scales, tab2_words, tab2_scales, offs, offs2, pos1, pos2,
              w1, w4_words, w4_scales, shade, gain, seamw, level):
    v = unpack_weight(tab_words, tab_scales, "e4m3")[:, unstriped(offs)]
    v2 = unpack_weight(tab2_words, tab2_scales, "e4m3")[:, unstriped(offs2)]
    w1q = mxq(f64(w1), 0, "e4m3")
    w4 = unpack_weight(w4_words, w4_scales, "e2m1")
    cloth = w1q.T @ v
    trim = w4.T @ v
    h = (cloth * f64(shade) + trim) * f64(gain)[:, None]
    x1 = mxq(np.abs(h[:, unstriped(pos1)]), 0, "e4m3")
    x2 = mxq(h[:, unstriped(pos2)], 0, "e4m3")
    e1 = v2.T @ x1
    e2 = v2.T @ x2
    out = e1 * f64(seamw)[:, None] + np.maximum(e2, f64(level)[:, None])
    return out

@@ -1,0 +1,314 @@
+from contextlib import ExitStack
+
+import concourse.mybir as mybir
+
+K, H, T, S, T3, S2, N = 1024, 512, 4096, 1024, 2048, 1024, 512
+FLOPS = 2 * (2 * K * H * S) + 2 * (2 * H * S2 * N)
+
+F32 = mybir.dt.float32
+BF16 = mybir.dt.bfloat16
+I32 = mybir.dt.int32
+U32 = mybir.dt.uint32
+U16 = mybir.dt.uint16
+U8 = mybir.dt.uint8
+FP8X4 = mybir.dt.float8_e4m3fn_x4
+FP4X4 = mybir.dt.float4_e2m1fn_x4
+ALU = mybir.AluOpType
+ACT = mybir.ActivationFunctionType
+
+P = 128
+PACK = 4
+PASSES = K // (P * PACK)
+BANK = 512
+HALVES = S // BANK
+M_TILES = S2 // P
+NH = N // 2
+LIST_ROWS = 16
+
+
+def tile_list_garment_decade_scores_kernel(
+    tc, tab_words, tab_scales, tab2_words, tab2_scales, offs, offs2, pos1, pos2,
+    w1, w4_words, w4_scales, shade, gain, seamw, level, out,
+):
+    nc = tc.nc
+    with ExitStack() as ctx:
+        keep = ctx.enter_context(tc.tile_pool(name="keep", bufs=1))
+        ring = ctx.enter_context(tc.tile_pool(name="ring", bufs=3))
+        psum = ctx.enter_context(tc.psum_pool(name="psum", bufs=8))
+
+        def held(shape, dtype, name, tag=None):
+            return keep.tile(shape, dtype, name=name, tag=tag or name, align_bytes=64)
+
+        v_scale_tab = held([P, T], U8, "v_scale_tab")
+        w4_scale_raw = held([P, PASSES * H], U8, "w4_scale_raw")
+        v2_scale_tab = held([P, T3], U8, "v2_scale_tab")
+        v_scale = held([P, PASSES * S], U8, "v_scale")
+        nc.vector.memset(w4_scale_raw[:].bitcast(I32), 0)
+        nc.vector.memset(v2_scale_tab[:].bitcast(I32), 0)
+        nc.vector.memset(v_scale_tab[32:64, :].bitcast(I32), 0)
+        nc.vector.memset(v_scale_tab[64:P, :].bitcast(I32), 0)
+        nc.vector.memset(v_scale[:].bitcast(I32), 0)
+
+        offs_t = held([P, S // LIST_ROWS], U16, "offs_t")
+        offs2_t = held([P, S2 // LIST_ROWS], U16, "offs2_t")
+        pos1_t = held([P, N // LIST_ROWS], U16, "pos1_t")
+        pos2_t = held([P, N // LIST_ROWS], U16, "pos2_t")
+        w4_raw = held([P, PASSES, H // 2], I32, "w4_raw")
+        gain_t = held([P, PACK], F32, "gain_t")
+        w1_raw = [held([P, PACK, H], F32, "w1_raw%d" % a) for a in range(PASSES)]
+        v_tab = [held([P, T], I32, "v_tab%d" % a) for a in range(PASSES)]
+
+        def load_w1(a):
+            nc.sync.dma_start(
+                w1_raw[a][:], w1[512 * a : 512 * (a + 1), :].rearrange("(p i) c -> p i c", i=PACK)
+            )
+
+        def load_v(a):
+            nc.sync.dma_start(v_tab[a][:], tab_words[a].rearrange("p t i -> p (t i)").bitcast(I32))
+
+        nc.sync.dma_start(offs_t[:], offs)
+        nc.sync.dma_start(
+            v_scale_tab[0:32, :].bitcast(I32), tab_scales.rearrange("a q t -> (a q) t").bitcast(I32)
+        )
+        nc.sync.dma_start(w4_raw[:], w4_words.rearrange("a p c -> p a c").bitcast(I32))
+        load_w1(0)
+        nc.sync.dma_start(offs2_t[:], offs2)
+        nc.sync.dma_start(gain_t[:], gain.rearrange("(p t) -> p t", t=PACK))
+        nc.sync.dma_start(pos1_t[:], pos1)
+        nc.sync.dma_start(pos2_t[:], pos2)
+        load_v(0)
+        for q in range(4):
+            nc.sync.dma_start(
+                w4_scale_raw[32 * q : 32 * q + 4, :].bitcast(I32).rearrange("r (a c) -> r a c", a=PASSES),
+                w4_scales[:, 4 * q : 4 * q + 4, :].rearrange("a r c -> r a c").bitcast(I32),
+            )
+        load_w1(1)
+        for q in range(4):
+            nc.sync.dma_start(
+                v2_scale_tab[32 * q : 32 * q + 4, :].bitcast(I32),
+                tab2_scales[0, 4 * q : 4 * q + 4, :].bitcast(I32),
+            )
+        load_v(1)
+
+        shade_rows = shade.rearrange("(p t) j -> p t j", t=PACK)
+        shade_t = {}
+        for pair in range(2):
+            for half in range(HALVES):
+                shade_t[pair, half] = held([P, 2, BANK], F32, "shade%d%d" % (pair, half), "shade%d%d" % (pair, half))
+                nc.sync.dma_start(
+                    shade_t[pair, half][:],
+                    shade_rows[:, 2 * pair : 2 * pair + 2, BANK * half : BANK * (half + 1)],
+                )
+        seamw_t = held([P, M_TILES], F32, "seamw_t")
+        level_t = held([P, M_TILES], F32, "level_t")
+        with nc.allow_non_contiguous_dma(reason="one value for each output row"):
+            nc.sync.dma_start(seamw_t[:], seamw.rearrange("(i p) -> p i", p=P))
+            nc.sync.dma_start(level_t[:], level.rearrange("(i p) -> p i", p=P))
+
+        v_scale_picked = held([P, S], U8, "v_scale_picked")
+        nc.vector.tensor_copy(out=v_scale_picked[:], in_=v_scale_tab[:].indirect(offs_t[:]))
+        for a in range(PASSES):
+            for q in range(4):
+                row = 16 * a + 4 * q
+                nc.gpsimd.dma_start(
+                    v_scale[32 * q : 32 * q + 4, S * a : S * (a + 1)].bitcast(I32),
+                    v_scale_picked[row : row + 4, :].bitcast(I32),
+                )
+
+        w4_codes = held([P, PASSES * H * 2], U8, "w4_codes")
+        nc.vector.tensor_copy(
+            out=w4_codes[:].bitcast(U16).rearrange("p (a t m) -> p a t m", a=PASSES, t=PACK),
+            in_=w4_raw[:].rearrange("p a c -> p (a c)").bitcast(U16).rearrange("p (a m t) -> p a t m", a=PASSES, t=PACK),
+        )
+
+        w1_codes, w1_scale = [], []
+
+        def quantize_w1(a):
+            grouped = held([P, PACK * H], BF16, "w1_grouped%d" % a)
+            nc.scalar.copy(
+                out=grouped[:].rearrange("p (t m i) -> p m i t", t=PACK, i=PACK),
+                in_=w1_raw[a][:].rearrange("p i (m t) -> p m i t", t=PACK),
+            )
+            w1_codes.append(held([P, H], U32, "w1_codes%d" % a))
+            w1_scale.append(held([P, H], U8, "w1_scale%d" % a))
+            nc.vector.quantize_mx(out=w1_codes[a][:].bitcast(FP8X4), scales=w1_scale[a][:], in_=grouped[:])
+
+        v_codes = {}
+
+        def gather_v(a):
+            for half in range(HALVES):
+                v_codes[a, half] = held([P, BANK], U32, "v_codes%d%d" % (a, half))
+                cols = BANK // LIST_ROWS
+                nc.vector.tensor_copy(
+                    out=v_codes[a, half][:],
+                    in_=v_tab[a][:].bitcast(U32).indirect(offs_t[:, cols * half : cols * (half + 1)]),
+                )
+
+        quantize_w1(0)
+        gather_v(0)
+        w4_scale = held([P, PASSES * H], U8, "w4_scale")
+        nc.vector.tensor_copy(
+            out=w4_scale[:].rearrange("p (a t m) -> p a t m", a=PASSES, t=PACK),
+            in_=w4_scale_raw[:].rearrange("p (a m t) -> p a t m", a=PASSES, t=PACK),
+        )
+        v2_scale = held([P, S2], U8, "v2_scale")
+        nc.vector.tensor_copy(out=v2_scale[:], in_=v2_scale_tab[:].indirect(offs2_t[:]))
+        quantize_w1(1)
+
+        def cloth_pass(acc, a, t, half):
+            cols = slice(S * a + BANK * half, S * a + BANK * (half + 1))
+            rows = slice(P * t, P * (t + 1))
+            nc.tensor.matmul_mx(
+                out=acc[:],
+                lhsT=w1_codes[a][:, rows].bitcast(FP8X4),
+                lhsT_scale=w1_scale[a][:, rows],
+                rhs=v_codes[a, half][:].bitcast(FP8X4),
+                rhs_scale=v_scale[:, cols],
+                start=(a == 0),
+                stop=(a == PASSES - 1),
+            )
+
+        def trim_pass(acc, a, t, half):
+            cols = slice(S * a + BANK * half, S * a + BANK * (half + 1))
+            first = H * a + P * t
+            nc.tensor.matmul_mx(
+                out=acc[:],
+                lhsT=w4_codes[:, 2 * first : 2 * (first + P)].bitcast(FP4X4),
+                lhsT_scale=w4_scale[:, first : first + P],
+                rhs=v_codes[a, half][:].bitcast(FP8X4),
+                rhs_scale=v_scale[:, cols],
+                start=(a == 0),
+                stop=(a == PASSES - 1),
+            )
+
+        h = [held([P, S], F32, "h%d" % t) for t in range(PACK)]
+
+        def combine(sums, pair, half):
+            shaded, summed = {}, {}
+            for u in range(2):
+                shaded[u] = ring.tile([P, BANK], F32, name="shaded")
+                nc.vector.tensor_tensor(
+                    out=shaded[u][:], in0=sums[2 * pair + u, half][0][:], in1=shade_t[pair, half][:, u, :], op=ALU.mult
+                )
+            for u in range(2):
+                summed[u] = ring.tile([P, BANK], F32, name="summed")
+                nc.vector.tensor_tensor(
+                    out=summed[u][:], in0=sums[2 * pair + u, half][1][:], in1=shaded[u][:], op=ALU.add
+                )
+            for u in range(2):
+                t = 2 * pair + u
+                nc.scalar.activation(
+                    out=h[t][:, BANK * half : BANK * (half + 1)], in_=summed[u][:], func=ACT.Copy,
+                    scale=gain_t[:, t : t + 1],
+                )
+
+        def open_sums(sums, pair, half):
+            for t in (2 * pair, 2 * pair + 1):
+                sums[t, half] = (
+                    psum.tile([P, BANK], F32, name="bank"),
+                    psum.tile([P, BANK], F32, name="bank"),
+                )
+
+        def passes(sums, pair, half, which):
+            for t in (2 * pair, 2 * pair + 1):
+                for a in which:
+                    cloth_pass(sums[t, half][0], a, t, half)
+            for t in (2 * pair, 2 * pair + 1):
+                for a in which:
+                    trim_pass(sums[t, half][1], a, t, half)
+
+        sums = {}
+        for half in range(HALVES):
+            open_sums(sums, 0, half)
+            passes(sums, 0, half, (0,))
+        gather_v(1)
+        for half in range(HALVES):
+            passes(sums, 0, half, (1,))
+        for half in range(HALVES):
+            combine(sums, 0, half)
+        v2_tab = held([P, T3], I32, "v2_tab", "shade01")
+        nc.sync.dma_start(v2_tab[:], tab2_words[0].rearrange("p t i -> p (t i)").bitcast(I32))
+        for half in range(HALVES):
+            open_sums(sums, 1, half)
+            passes(sums, 1, half, (0, 1))
+            combine(sums, 1, half)
+
+        def pick(name, tag, offsets, width):
+            picked = held([P, PACK, width], F32, name, tag)
+            for t in range(PACK):
+                nc.vector.tensor_copy(out=picked[:, t, :], in_=h[t][:].indirect(offsets))
+            return picked
+
+        def interleave(name, tag, picked, func, width):
+            grouped = held([P, PACK * width], BF16, name, tag)
+            nc.scalar.activation(
+                out=grouped[:].rearrange("p (c i t) -> p c t i", i=4, t=PACK),
+                in_=picked[:].rearrange("p t (c i) -> p c t i", i=4),
+                func=func,
+            )
+            return grouped
+
+        def quantize(name, grouped, width):
+            codes = held([P, width], U32, name + "_codes")
+            scale = held([P, width], U8, name + "_scale")
+            nc.vector.quantize_mx(out=codes[:].bitcast(FP8X4), scales=scale[:], in_=grouped[:])
+            return codes, scale
+
+        def scores(acc, i, x):
+            rows = slice(P * i, P * (i + 1))
+            nc.tensor.matmul_mx(
+                out=acc,
+                lhsT=v2_codes[:, rows].bitcast(FP8X4),
+                lhsT_scale=v2_scale[:, rows],
+                rhs=x[0][:].bitcast(FP8X4),
+                rhs_scale=x[1][:],
+                start=True,
+                stop=True,
+            )
+
+        v2_codes = held([P, S2], U32, "v2_codes")
+        nc.vector.tensor_copy(out=v2_codes[:], in_=v2_tab[:].bitcast(U32).indirect(offs2_t[:]))
+        cols = NH // LIST_ROWS
+        picked1 = pick("picked1", None, pos1_t[:], N)
+        grouped1 = interleave("grouped1", "reused", picked1, ACT.Abs, N)
+        picked2a = pick("picked2a", None, pos2_t[:, 0:cols], NH)
+        x1 = quantize("x1", grouped1, N)
+        grouped2a = interleave("grouped2a", None, picked2a, ACT.Copy, NH)
+        picked2b = pick("picked2b", "reused", pos2_t[:, cols : 2 * cols], NH)
+
+        seam = [held([P, N], F32, "seam%d" % i) for i in range(M_TILES)]
+
+        def seam_scores(tiles):
+            for i in tiles:
+                acc = psum.tile([P, BANK], F32, name="bank")
+                scores(acc[:], i, x1)
+                nc.scalar.activation(out=seam[i][:], in_=acc[:], func=ACT.Copy, scale=seamw_t[:, i : i + 1])
+
+        seam_scores(range(0, 3))
+        grouped2b = interleave("grouped2b", None, picked2b, ACT.Copy, NH)
+        seam_scores(range(3, 8))
+
+        out_rows = out.rearrange("(i p) n -> p i n", p=P)
+
+        def finish(x2, half, pairs):
+            for pair in pairs:
+                acc = psum.tile([P, 2, NH], F32, name="bank")
+                for u in range(2):
+                    scores(acc[:, u, :], 2 * pair + u, x2)
+                result = held([P, 2, NH], F32, "result%d%d" % (half, pair))
+                for u in range(2):
+                    i = 2 * pair + u
+                    nc.vector.scalar_tensor_tensor(
+                        out=result[:, u, :], in0=acc[:, u, :], scalar=level_t[:, i : i + 1],
+                        in1=seam[i][:, NH * half : NH * (half + 1)], op0=ALU.max, op1=ALU.add,
+                    )
+                nc.sync.dma_start(out_rows[:, 2 * pair : 2 * pair + 2, NH * half : NH * (half + 1)], result[:])
+
+        x2a = quantize("x2a", grouped2a, NH)
+        finish(x2a, 0, range(0, 2))
+        x2b = quantize("x2b", grouped2b, NH)
+        finish(x2b, 1, range(0, 1))
+        finish(x2a, 0, range(2, 3))
+        finish(x2b, 1, range(1, 2))
+        finish(x2a, 0, range(3, 4))
+        finish(x2b, 1, range(2, 4))

@@ -1,6 +1,7 @@
 from contextlib import ExitStack
 
 import concourse.mybir as mybir
+from concourse.masks import make_identity
 
 K, H, T, S, T3, S2, N = 1024, 512, 4096, 1024, 2048, 1024, 512
 FLOPS = 2 * (2 * K * H * S) + 2 * (2 * H * S2 * N)
@@ -33,21 +34,27 @@ def tile_list_garment_decade_scores_kernel(
     nc = tc.nc
     with ExitStack() as ctx:
         keep = ctx.enter_context(tc.tile_pool(name="keep", bufs=1))
-        ring = ctx.enter_context(tc.tile_pool(name="ring", bufs=3))
+        ring = ctx.enter_context(tc.tile_pool(name="ring", bufs=4))
         psum = ctx.enter_context(tc.psum_pool(name="psum", bufs=8))
 
         def held(shape, dtype, name, tag=None):
             return keep.tile(shape, dtype, name=name, tag=tag or name, align_bytes=64)
 
-        v_scale_tab = held([P, T], U8, "v_scale_tab")
         w4_scale_raw = held([P, PASSES * H], U8, "w4_scale_raw")
         v2_scale_tab = held([P, T3], U8, "v2_scale_tab")
-        v_scale = held([P, PASSES * S], U8, "v_scale")
+        v_scale_tab = held([P, T], U8, "v_scale_tab")
         nc.vector.memset(w4_scale_raw[:].bitcast(I32), 0)
         nc.vector.memset(v2_scale_tab[:].bitcast(I32), 0)
-        nc.vector.memset(v_scale_tab[32:64, :].bitcast(I32), 0)
-        nc.vector.memset(v_scale_tab[64:P, :].bitcast(I32), 0)
-        nc.vector.memset(v_scale[:].bitcast(I32), 0)
+        nc.vector.memset(v_scale_tab[0:96, :].bitcast(I32), 0)
+        v_scale = held([P, PASSES * S], U8, "v_scale")
+        nc.gpsimd.memset(v_scale[:].bitcast(I32), 0)
+
+        identity = held([P, P], F32, "identity")
+        row_consts = held([P, P], F32, "row_consts")
+        nc.gpsimd.memset(row_consts[:], 0.0)
+        nc.gpsimd.dma_start(row_consts[0:M_TILES, :], seamw.rearrange("(i p) -> i p", p=P))
+        nc.gpsimd.dma_start(row_consts[M_TILES : 2 * M_TILES, :], level.rearrange("(i p) -> i p", p=P))
+        make_identity(nc, identity[:])
 
         offs_t = held([P, S // LIST_ROWS], U16, "offs_t")
         offs2_t = held([P, S2 // LIST_ROWS], U16, "offs2_t")
@@ -55,62 +62,40 @@ def tile_list_garment_decade_scores_kernel(
         pos2_t = held([P, N // LIST_ROWS], U16, "pos2_t")
         w4_raw = held([P, PASSES, H // 2], I32, "w4_raw")
         gain_t = held([P, PACK], F32, "gain_t")
-        w1_raw = [held([P, PACK, H], F32, "w1_raw%d" % a) for a in range(PASSES)]
-        v_tab = [held([P, T], I32, "v_tab%d" % a) for a in range(PASSES)]
 
-        def load_w1(a):
-            nc.sync.dma_start(
-                w1_raw[a][:], w1[512 * a : 512 * (a + 1), :].rearrange("(p i) c -> p i c", i=PACK)
-            )
-
-        def load_v(a):
-            nc.sync.dma_start(v_tab[a][:], tab_words[a].rearrange("p t i -> p (t i)").bitcast(I32))
+        def load_v(tile, a, part):
+            cols = slice(T // 2 * part, T // 2 * (part + 1))
+            nc.sync.dma_start(tile[:, cols], tab_words[a].rearrange("p t i -> p (t i)").bitcast(I32)[:, cols])
 
         nc.sync.dma_start(offs_t[:], offs)
         nc.sync.dma_start(
-            v_scale_tab[0:32, :].bitcast(I32), tab_scales.rearrange("a q t -> (a q) t").bitcast(I32)
+            v_scale_tab[96:P, :].bitcast(I32), tab_scales.rearrange("a q t -> (a q) t").bitcast(I32)
         )
         nc.sync.dma_start(w4_raw[:], w4_words.rearrange("a p c -> p a c").bitcast(I32))
-        load_w1(0)
+        w1_raw0 = held([P, PACK, H], F32, "w1_raw0")
+        nc.sync.dma_start(w1_raw0[:], w1[0:512, :].rearrange("(p i) c -> p i c", i=PACK))
         nc.sync.dma_start(offs2_t[:], offs2)
-        nc.sync.dma_start(gain_t[:], gain.rearrange("(p t) -> p t", t=PACK))
-        nc.sync.dma_start(pos1_t[:], pos1)
-        nc.sync.dma_start(pos2_t[:], pos2)
-        load_v(0)
         for q in range(4):
             nc.sync.dma_start(
                 w4_scale_raw[32 * q : 32 * q + 4, :].bitcast(I32).rearrange("r (a c) -> r a c", a=PASSES),
                 w4_scales[:, 4 * q : 4 * q + 4, :].rearrange("a r c -> r a c").bitcast(I32),
             )
-        load_w1(1)
+        v_tab0 = held([P, T], I32, "v_tab0")
+        load_v(v_tab0, 0, 0)
         for q in range(4):
             nc.sync.dma_start(
                 v2_scale_tab[32 * q : 32 * q + 4, :].bitcast(I32),
                 tab2_scales[0, 4 * q : 4 * q + 4, :].bitcast(I32),
             )
-        load_v(1)
-
-        shade_rows = shade.rearrange("(p t) j -> p t j", t=PACK)
-        shade_t = {}
-        for pair in range(2):
-            for half in range(HALVES):
-                shade_t[pair, half] = held([P, 2, BANK], F32, "shade%d%d" % (pair, half), "shade%d%d" % (pair, half))
-                nc.sync.dma_start(
-                    shade_t[pair, half][:],
-                    shade_rows[:, 2 * pair : 2 * pair + 2, BANK * half : BANK * (half + 1)],
-                )
-        seamw_t = held([P, M_TILES], F32, "seamw_t")
-        level_t = held([P, M_TILES], F32, "level_t")
-        with nc.allow_non_contiguous_dma(reason="one value for each output row"):
-            nc.sync.dma_start(seamw_t[:], seamw.rearrange("(i p) -> p i", p=P))
-            nc.sync.dma_start(level_t[:], level.rearrange("(i p) -> p i", p=P))
+        load_v(v_tab0, 0, 1)
 
         v_scale_picked = held([P, S], U8, "v_scale_picked")
         nc.vector.tensor_copy(out=v_scale_picked[:], in_=v_scale_tab[:].indirect(offs_t[:]))
-        for a in range(PASSES):
+
+        def move_v_scale(a):
             for q in range(4):
-                row = 16 * a + 4 * q
-                nc.gpsimd.dma_start(
+                row = 96 + 16 * a + 4 * q
+                nc.sync.dma_start(
                     v_scale[32 * q : 32 * q + 4, S * a : S * (a + 1)].bitcast(I32),
                     v_scale_picked[row : row + 4, :].bitcast(I32),
                 )
@@ -121,31 +106,44 @@ def tile_list_garment_decade_scores_kernel(
             in_=w4_raw[:].rearrange("p a c -> p (a c)").bitcast(U16).rearrange("p (a m t) -> p a t m", a=PASSES, t=PACK),
         )
 
-        w1_codes, w1_scale = [], []
+        w1_codes = [held([P, H], U32, "w1_codes%d" % a) for a in range(PASSES)]
+        w1_scale = [held([P, H], U8, "w1_scale%d" % a) for a in range(PASSES)]
 
-        def quantize_w1(a):
-            grouped = held([P, PACK * H], BF16, "w1_grouped%d" % a)
-            nc.scalar.copy(
-                out=grouped[:].rearrange("p (t m i) -> p m i t", t=PACK, i=PACK),
-                in_=w1_raw[a][:].rearrange("p i (m t) -> p m i t", t=PACK),
+        def regroup_w1(copy, grouped, raw, first, count, offset):
+            copy(
+                out=grouped[:].rearrange("p (t m i) -> p m i t", t=PACK, i=PACK)[:, first : first + count],
+                in_=raw[:].rearrange("p i (m t) -> p m i t", t=PACK)[:, first - offset : first - offset + count],
             )
-            w1_codes.append(held([P, H], U32, "w1_codes%d" % a))
-            w1_scale.append(held([P, H], U8, "w1_scale%d" % a))
-            nc.vector.quantize_mx(out=w1_codes[a][:].bitcast(FP8X4), scales=w1_scale[a][:], in_=grouped[:])
+
+        def quantize_w1_first(raw):
+            grouped = held([P, PACK * H], BF16, "w1_grouped0")
+            regroup_w1(nc.scalar.copy, grouped, raw, 0, P, 0)
+            nc.vector.quantize_mx(out=w1_codes[0][:].bitcast(FP8X4), scales=w1_scale[0][:], in_=grouped[:])
+
+        def quantize_w1_last(parts):
+            grouped = held([P, PACK * H], BF16, "w1_grouped1")
+            regroup_w1(nc.scalar.copy, grouped, parts[0], 0, 64, 0)
+            regroup_w1(nc.scalar.copy, grouped, parts[1], 64, 32, 64)
+            regroup_w1(nc.vector.tensor_copy, grouped, parts[1], 96, 32, 64)
+            for pair in range(2):
+                cols = slice(2 * P * pair, 2 * P * (pair + 1))
+                nc.vector.quantize_mx(
+                    out=w1_codes[1][:, cols].bitcast(FP8X4), scales=w1_scale[1][:, cols],
+                    in_=grouped[:, 8 * P * pair : 8 * P * (pair + 1)],
+                )
 
         v_codes = {}
 
-        def gather_v(a):
+        def gather_v(a, tile):
             for half in range(HALVES):
                 v_codes[a, half] = held([P, BANK], U32, "v_codes%d%d" % (a, half))
                 cols = BANK // LIST_ROWS
                 nc.vector.tensor_copy(
                     out=v_codes[a, half][:],
-                    in_=v_tab[a][:].bitcast(U32).indirect(offs_t[:, cols * half : cols * (half + 1)]),
+                    in_=tile[:].bitcast(U32).indirect(offs_t[:, cols * half : cols * (half + 1)]),
                 )
 
-        quantize_w1(0)
-        gather_v(0)
+        quantize_w1_first(w1_raw0)
         w4_scale = held([P, PASSES * H], U8, "w4_scale")
         nc.vector.tensor_copy(
             out=w4_scale[:].rearrange("p (a t m) -> p a t m", a=PASSES, t=PACK),
@@ -153,7 +151,43 @@ def tile_list_garment_decade_scores_kernel(
         )
         v2_scale = held([P, S2], U8, "v2_scale")
         nc.vector.tensor_copy(out=v2_scale[:], in_=v2_scale_tab[:].indirect(offs2_t[:]))
-        quantize_w1(1)
+        gather_v(0, v_tab0)
+
+        v_tab1 = held([P, T], I32, "v_tab1", "v_scale_tab")
+        load_v(v_tab1, 1, 0)
+        move_v_scale(0)
+        load_v(v_tab1, 1, 1)
+        move_v_scale(1)
+        w1_last = []
+        for part, tag in enumerate(("w1_raw0", "w1_grouped0")):
+            w1_last.append(held([P, PACK, H // 2], F32, "w1_last%d" % part, tag))
+            nc.sync.dma_start(
+                w1_last[part][:],
+                w1[512:1024, H // 2 * part : H // 2 * (part + 1)].rearrange("(p i) c -> p i c", i=PACK),
+            )
+
+        shade_rows = shade.rearrange("(p t) j -> p t j", t=PACK)
+        shade_t = {}
+
+        def load_shade(pair, half, tag):
+            shade_t[pair, half] = held([P, 2, BANK], F32, "shade%d%d" % (pair, half), tag)
+            nc.sync.dma_start(
+                shade_t[pair, half][:],
+                shade_rows[:, 2 * pair : 2 * pair + 2, BANK * half : BANK * (half + 1)],
+            )
+
+        load_shade(0, 0, "w4_scale_raw")
+        load_shade(0, 1, "v2_scale_tab")
+        load_shade(1, 0, "v_tab0")
+        load_shade(1, 1, "v_scale_picked")
+        nc.sync.dma_start(gain_t[:], gain.rearrange("(p t) -> p t", t=PACK))
+        nc.sync.dma_start(pos1_t[:], pos1)
+        nc.sync.dma_start(pos2_t[:], pos2)
+
+        turned = psum.tile([P, P], F32, name="bank")
+        nc.tensor.transpose(turned[:], row_consts[:], identity[:])
+        col_consts = held([P, 2 * M_TILES], F32, "col_consts")
+        nc.scalar.copy(out=col_consts[:], in_=turned[:, 0 : 2 * M_TILES])
 
         def cloth_pass(acc, a, t, half):
             cols = slice(S * a + BANK * half, S * a + BANK * (half + 1))
@@ -183,22 +217,31 @@ def tile_list_garment_decade_scores_kernel(
 
         h = [held([P, S], F32, "h%d" % t) for t in range(PACK)]
 
-        def combine(sums, pair, half):
-            shaded, summed = {}, {}
+        summed_t = [held([P, PACK, BANK], F32, "summed%d" % half) for half in range(HALVES)]
+
+        def combine(sums, pair, half, trim_out=None):
+            shaded = [ring.tile([P, BANK], F32, name="shaded") for u in range(2)]
+            summed = summed_t[half][:, 2 * pair : 2 * pair + 2, :]
             for u in range(2):
-                shaded[u] = ring.tile([P, BANK], F32, name="shaded")
                 nc.vector.tensor_tensor(
                     out=shaded[u][:], in0=sums[2 * pair + u, half][0][:], in1=shade_t[pair, half][:, u, :], op=ALU.mult
                 )
             for u in range(2):
-                summed[u] = ring.tile([P, BANK], F32, name="summed")
-                nc.vector.tensor_tensor(
-                    out=summed[u][:], in0=sums[2 * pair + u, half][1][:], in1=shaded[u][:], op=ALU.add
-                )
+                trim = sums[2 * pair + u, half][1]
+                if trim_out is not None:
+                    nc.scalar.copy(out=trim_out[:, 2 * half + u, :], in_=trim[:])
+                    nc.gpsimd.tensor_tensor(
+                        out=summed[:, u, :], in0=trim_out[:, 2 * half + u, :], in1=shaded[u][:], op=ALU.add
+                    )
+                else:
+                    nc.vector.tensor_tensor(out=summed[:, u, :], in0=trim[:], in1=shaded[u][:], op=ALU.add)
+            return summed
+
+        def apply_gain(summed, pair, half):
             for u in range(2):
                 t = 2 * pair + u
                 nc.scalar.activation(
-                    out=h[t][:, BANK * half : BANK * (half + 1)], in_=summed[u][:], func=ACT.Copy,
+                    out=h[t][:, BANK * half : BANK * (half + 1)], in_=summed[:, u, :], func=ACT.Copy,
                     scale=gain_t[:, t : t + 1],
                 )
 
@@ -209,29 +252,35 @@ def tile_list_garment_decade_scores_kernel(
                     psum.tile([P, BANK], F32, name="bank"),
                 )
 
-        def passes(sums, pair, half, which):
+        def passes(one_pass, side, sums, pair, half, which):
             for t in (2 * pair, 2 * pair + 1):
                 for a in which:
-                    cloth_pass(sums[t, half][0], a, t, half)
-            for t in (2 * pair, 2 * pair + 1):
-                for a in which:
-                    trim_pass(sums[t, half][1], a, t, half)
+                    one_pass(sums[t, half][side], a, t, half)
 
         sums = {}
         for half in range(HALVES):
             open_sums(sums, 0, half)
-            passes(sums, 0, half, (0,))
-        gather_v(1)
-        for half in range(HALVES):
-            passes(sums, 0, half, (1,))
-        for half in range(HALVES):
-            combine(sums, 0, half)
-        v2_tab = held([P, T3], I32, "v2_tab", "shade01")
+            passes(cloth_pass, 0, sums, 0, half, (0,))
+            passes(trim_pass, 1, sums, 0, half, (0,))
+        gather_v(1, v_tab1)
+        v2_tab = held([P, T3], I32, "v2_tab", "v_scale_tab")
         nc.sync.dma_start(v2_tab[:], tab2_words[0].rearrange("p t i -> p (t i)").bitcast(I32))
+        quantize_w1_last(w1_last)
+        for half in range(HALVES):
+            passes(cloth_pass, 0, sums, 0, half, (1,))
+        for half in range(HALVES):
+            passes(trim_pass, 1, sums, 0, half, (1,))
+        trim_out = held([P, 2 * HALVES, BANK], F32, "trim_out", "w1_grouped0")
+        summed = [combine(sums, 0, half, trim_out) for half in range(HALVES)]
+        for half in range(HALVES):
+            apply_gain(summed[half], 0, half)
         for half in range(HALVES):
             open_sums(sums, 1, half)
-            passes(sums, 1, half, (0, 1))
-            combine(sums, 1, half)
+            passes(cloth_pass, 0, sums, 1, half, (0, 1))
+            passes(trim_pass, 1, sums, 1, half, (0, 1))
+            apply_gain(combine(sums, 1, half), 1, half)
+        v2_codes = held([P, S2], U32, "v2_codes")
+        nc.vector.tensor_copy(out=v2_codes[:], in_=v2_tab[:].bitcast(U32).indirect(offs2_t[:]))
 
         def pick(name, tag, offsets, width):
             picked = held([P, PACK, width], F32, name, tag)
@@ -266,15 +315,17 @@ def tile_list_garment_decade_scores_kernel(
                 stop=True,
             )
 
-        v2_codes = held([P, S2], U32, "v2_codes")
-        nc.vector.tensor_copy(out=v2_codes[:], in_=v2_tab[:].bitcast(U32).indirect(offs2_t[:]))
         cols = NH // LIST_ROWS
         picked1 = pick("picked1", None, pos1_t[:], N)
         grouped1 = interleave("grouped1", "reused", picked1, ACT.Abs, N)
-        picked2a = pick("picked2a", None, pos2_t[:, 0:cols], NH)
+        picked2a = pick("picked2a", "summed1", pos2_t[:, 0:cols], NH)
         x1 = quantize("x1", grouped1, N)
         grouped2a = interleave("grouped2a", None, picked2a, ACT.Copy, NH)
-        picked2b = pick("picked2b", "reused", pos2_t[:, cols : 2 * cols], NH)
+        picked2b = held([P, PACK, NH], F32, "picked2b", "reused")
+        for t in range(PACK):
+            nc.vector.tensor_copy(out=picked2b[:, t, :], in_=h[t][:].indirect(pos2_t[:, cols : 2 * cols]))
+            if t == 1:
+                x2a = quantize("x2a", grouped2a, NH)
 
         seam = [held([P, N], F32, "seam%d" % i) for i in range(M_TILES)]
 
@@ -282,33 +333,43 @@ def tile_list_garment_decade_scores_kernel(
             for i in tiles:
                 acc = psum.tile([P, BANK], F32, name="bank")
                 scores(acc[:], i, x1)
-                nc.scalar.activation(out=seam[i][:], in_=acc[:], func=ACT.Copy, scale=seamw_t[:, i : i + 1])
+                nc.scalar.activation(out=seam[i][:], in_=acc[:], func=ACT.Copy, scale=col_consts[:, i : i + 1])
 
-        seam_scores(range(0, 3))
+        seam_scores(range(0, 4))
         grouped2b = interleave("grouped2b", None, picked2b, ACT.Copy, NH)
-        seam_scores(range(3, 8))
+        seam_scores(range(4, 8))
 
         out_rows = out.rearrange("(i p) n -> p i n", p=P)
 
-        def finish(x2, half, pairs):
-            for pair in pairs:
-                acc = psum.tile([P, 2, NH], F32, name="bank")
-                for u in range(2):
-                    scores(acc[:, u, :], 2 * pair + u, x2)
-                result = held([P, 2, NH], F32, "result%d%d" % (half, pair))
-                for u in range(2):
-                    i = 2 * pair + u
-                    nc.vector.scalar_tensor_tensor(
-                        out=result[:, u, :], in0=acc[:, u, :], scalar=level_t[:, i : i + 1],
-                        in1=seam[i][:, NH * half : NH * (half + 1)], op0=ALU.max, op1=ALU.add,
-                    )
-                nc.sync.dma_start(out_rows[:, 2 * pair : 2 * pair + 2, NH * half : NH * (half + 1)], result[:])
+        def finish(result, acc, i, cols):
+            nc.vector.scalar_tensor_tensor(
+                out=result, in0=acc, scalar=col_consts[:, M_TILES + i : M_TILES + i + 1],
+                in1=seam[i][:, cols], op0=ALU.max, op1=ALU.add,
+            )
 
-        x2a = quantize("x2a", grouped2a, NH)
-        finish(x2a, 0, range(0, 2))
-        x2b = quantize("x2b", grouped2b, NH)
-        finish(x2b, 1, range(0, 1))
-        finish(x2a, 0, range(2, 3))
-        finish(x2b, 1, range(1, 2))
-        finish(x2a, 0, range(3, 4))
-        finish(x2b, 1, range(2, 4))
+        def half_scores(x2, pair):
+            acc = psum.tile([P, 2, NH], F32, name="bank")
+            for u in range(2):
+                scores(acc[:, u, :], 2 * pair + u, x2)
+            return acc
+
+        def finish_half(acc, half, pair, between=None):
+            cols = slice(NH * half, NH * (half + 1))
+            result = held([P, 2, NH], F32, "result%d%d" % (half, pair))
+            finish(result[:, 0, :], acc[:, 0, :], 2 * pair, cols)
+            made = between() if between else None
+            finish(result[:, 1, :], acc[:, 1, :], 2 * pair + 1, cols)
+            nc.sync.dma_start(out_rows[:, 2 * pair : 2 * pair + 2, cols], result[:])
+            return made
+
+        finish_half(half_scores(x2a, 0), 0, 0)
+        x2b = finish_half(half_scores(x2a, 1), 0, 1, lambda: quantize("x2b", grouped2b, NH))
+        for pair in range(2):
+            finish_half(half_scores(x2b, pair), 1, pair)
+        for i in range(4, M_TILES):
+            acc = psum.tile([P, 2, NH], F32, name="bank")
+            scores(acc[:, 0, :], i, x2a)
+            scores(acc[:, 1, :], i, x2b)
+            result = held([P, N], F32, "result%d" % i)
+            finish(result[:], acc[:].rearrange("p u n -> p (u n)"), i, slice(0, N))
+            nc.sync.dma_start(out_rows[:, i, :], result[:])

@@ -25,6 +25,7 @@ HALVES = S // BANK
 M_TILES = S2 // P
 NH = N // 2
 LIST_ROWS = 16
+GPSIMD_SUMS = 5
 
 
 def tile_list_garment_decade_scores_kernel(
@@ -34,7 +35,7 @@ def tile_list_garment_decade_scores_kernel(
     nc = tc.nc
     with ExitStack() as ctx:
         keep = ctx.enter_context(tc.tile_pool(name="keep", bufs=1))
-        ring = ctx.enter_context(tc.tile_pool(name="ring", bufs=4))
+        ring = ctx.enter_context(tc.tile_pool(name="ring", bufs=6))
         psum = ctx.enter_context(tc.psum_pool(name="psum", bufs=8))
 
         def held(shape, dtype, name, tag=None):
@@ -75,29 +76,25 @@ def tile_list_garment_decade_scores_kernel(
         w1_raw0 = held([P, PACK, H], F32, "w1_raw0")
         nc.sync.dma_start(w1_raw0[:], w1[0:512, :].rearrange("(p i) c -> p i c", i=PACK))
         nc.sync.dma_start(offs2_t[:], offs2)
-        for q in range(4):
+        for r in range(4):
             nc.sync.dma_start(
-                w4_scale_raw[32 * q : 32 * q + 4, :].bitcast(I32).rearrange("r (a c) -> r a c", a=PASSES),
-                w4_scales[:, 4 * q : 4 * q + 4, :].rearrange("a r c -> r a c").bitcast(I32),
+                w4_scale_raw[r:P:32, :].bitcast(I32).rearrange("q (a c) -> q a c", a=PASSES),
+                w4_scales.rearrange("a (q r) c -> r q a c", r=4)[r].bitcast(I32),
             )
         v_tab0 = held([P, T], I32, "v_tab0")
         load_v(v_tab0, 0, 0)
-        for q in range(4):
-            nc.sync.dma_start(
-                v2_scale_tab[32 * q : 32 * q + 4, :].bitcast(I32),
-                tab2_scales[0, 4 * q : 4 * q + 4, :].bitcast(I32),
-            )
+        nc.sync.dma_start(v2_scale_tab[4:20, :].bitcast(I32), tab2_scales[0].bitcast(I32))
         load_v(v_tab0, 0, 1)
 
         v_scale_picked = held([P, S], U8, "v_scale_picked")
         nc.vector.tensor_copy(out=v_scale_picked[:], in_=v_scale_tab[:].indirect(offs_t[:]))
 
         def move_v_scale(a):
-            for q in range(4):
-                row = 96 + 16 * a + 4 * q
+            for r in range(4):
+                row = 96 + 16 * a
                 nc.sync.dma_start(
-                    v_scale[32 * q : 32 * q + 4, S * a : S * (a + 1)].bitcast(I32),
-                    v_scale_picked[row : row + 4, :].bitcast(I32),
+                    v_scale[r:P:32, S * a : S * (a + 1)].bitcast(I32),
+                    v_scale_picked[row + r : row + 16 : 4, :].bitcast(I32),
                 )
 
         w4_codes = held([P, PASSES * H * 2], U8, "w4_codes")
@@ -125,11 +122,10 @@ def tile_list_garment_decade_scores_kernel(
             regroup_w1(nc.scalar.copy, grouped, parts[0], 0, 64, 0)
             regroup_w1(nc.scalar.copy, grouped, parts[1], 64, 32, 64)
             regroup_w1(nc.vector.tensor_copy, grouped, parts[1], 96, 32, 64)
-            for pair in range(2):
-                cols = slice(2 * P * pair, 2 * P * (pair + 1))
+            for first, last in ((0, P), (P, 2 * P), (2 * P, H)):
                 nc.vector.quantize_mx(
-                    out=w1_codes[1][:, cols].bitcast(FP8X4), scales=w1_scale[1][:, cols],
-                    in_=grouped[:, 8 * P * pair : 8 * P * (pair + 1)],
+                    out=w1_codes[1][:, first:last].bitcast(FP8X4), scales=w1_scale[1][:, first:last],
+                    in_=grouped[:, PACK * first : PACK * last],
                 )
 
         v_codes = {}
@@ -149,8 +145,8 @@ def tile_list_garment_decade_scores_kernel(
             out=w4_scale[:].rearrange("p (a t m) -> p a t m", a=PASSES, t=PACK),
             in_=w4_scale_raw[:].rearrange("p (a m t) -> p a t m", a=PASSES, t=PACK),
         )
-        v2_scale = held([P, S2], U8, "v2_scale")
-        nc.vector.tensor_copy(out=v2_scale[:], in_=v2_scale_tab[:].indirect(offs2_t[:]))
+        v2_scale_picked = held([P, S2], U8, "v2_scale_picked")
+        nc.vector.tensor_copy(out=v2_scale_picked[:], in_=v2_scale_tab[:].indirect(offs2_t[:]))
         gather_v(0, v_tab0)
 
         v_tab1 = held([P, T], I32, "v_tab1", "v_scale_tab")
@@ -159,7 +155,7 @@ def tile_list_garment_decade_scores_kernel(
         load_v(v_tab1, 1, 1)
         move_v_scale(1)
         w1_last = []
-        for part, tag in enumerate(("w1_raw0", "w1_grouped0")):
+        for part, tag in enumerate(("w4_raw", "w4_scale_raw")):
             w1_last.append(held([P, PACK, H // 2], F32, "w1_last%d" % part, tag))
             nc.sync.dma_start(
                 w1_last[part][:],
@@ -167,19 +163,10 @@ def tile_list_garment_decade_scores_kernel(
             )
 
         shade_rows = shade.rearrange("(p t) j -> p t j", t=PACK)
-        shade_t = {}
-
-        def load_shade(pair, half, tag):
-            shade_t[pair, half] = held([P, 2, BANK], F32, "shade%d%d" % (pair, half), tag)
-            nc.sync.dma_start(
-                shade_t[pair, half][:],
-                shade_rows[:, 2 * pair : 2 * pair + 2, BANK * half : BANK * (half + 1)],
-            )
-
-        load_shade(0, 0, "w4_scale_raw")
-        load_shade(0, 1, "v2_scale_tab")
-        load_shade(1, 0, "v_tab0")
-        load_shade(1, 1, "v_scale_picked")
+        shade_t = []
+        for t, tag in enumerate(("w1_raw0", "w1_grouped0", "v_tab0", "v_scale_picked")):
+            shade_t.append(held([P, S], F32, "shade%d" % t, tag))
+            nc.sync.dma_start(shade_t[t][:], shade_rows[:, t, :])
         nc.sync.dma_start(gain_t[:], gain.rearrange("(p t) -> p t", t=PACK))
         nc.sync.dma_start(pos1_t[:], pos1)
         nc.sync.dma_start(pos2_t[:], pos2)
@@ -217,68 +204,75 @@ def tile_list_garment_decade_scores_kernel(
 
         h = [held([P, S], F32, "h%d" % t) for t in range(PACK)]
 
-        summed_t = [held([P, PACK, BANK], F32, "summed%d" % half) for half in range(HALVES)]
+        summed = [held([P, PACK, BANK], F32, "summed%d" % half) for half in range(HALVES)]
 
-        def combine(sums, pair, half, trim_out=None):
-            shaded = [ring.tile([P, BANK], F32, name="shaded") for u in range(2)]
-            summed = summed_t[half][:, 2 * pair : 2 * pair + 2, :]
-            for u in range(2):
+        def combine(t):
+            shaded = [ring.tile([P, BANK], F32, name="shaded") for half in range(HALVES)]
+            for half in range(HALVES):
                 nc.vector.tensor_tensor(
-                    out=shaded[u][:], in0=sums[2 * pair + u, half][0][:], in1=shade_t[pair, half][:, u, :], op=ALU.mult
+                    out=shaded[half][:], in0=sums[t, half][0][:],
+                    in1=shade_t[t][:, BANK * half : BANK * (half + 1)], op=ALU.mult,
                 )
-            for u in range(2):
-                trim = sums[2 * pair + u, half][1]
-                if trim_out is not None:
-                    nc.scalar.copy(out=trim_out[:, 2 * half + u, :], in_=trim[:])
+            for half in range(HALVES):
+                trim = sums[t, half][1]
+                place = HALVES * t + half
+                if place < GPSIMD_SUMS:
+                    nc.scalar.copy(out=trim_out[:, place, :], in_=trim[:])
                     nc.gpsimd.tensor_tensor(
-                        out=summed[:, u, :], in0=trim_out[:, 2 * half + u, :], in1=shaded[u][:], op=ALU.add
+                        out=summed[half][:, t, :], in0=trim_out[:, place, :], in1=shaded[half][:], op=ALU.add
                     )
                 else:
-                    nc.vector.tensor_tensor(out=summed[:, u, :], in0=trim[:], in1=shaded[u][:], op=ALU.add)
-            return summed
+                    nc.vector.tensor_tensor(out=summed[half][:, t, :], in0=trim[:], in1=shaded[half][:], op=ALU.add)
 
-        def apply_gain(summed, pair, half):
-            for u in range(2):
-                t = 2 * pair + u
+        def apply_gain(t):
+            for half in range(HALVES):
                 nc.scalar.activation(
-                    out=h[t][:, BANK * half : BANK * (half + 1)], in_=summed[:, u, :], func=ACT.Copy,
+                    out=h[t][:, BANK * half : BANK * (half + 1)], in_=summed[half][:, t, :], func=ACT.Copy,
                     scale=gain_t[:, t : t + 1],
                 )
 
-        def open_sums(sums, pair, half):
-            for t in (2 * pair, 2 * pair + 1):
+        sums = {}
+
+        def open_sums(t):
+            for half in range(HALVES):
                 sums[t, half] = (
                     psum.tile([P, BANK], F32, name="bank"),
                     psum.tile([P, BANK], F32, name="bank"),
                 )
 
-        def passes(one_pass, side, sums, pair, half, which):
-            for t in (2 * pair, 2 * pair + 1):
+        def passes(one_pass, side, t, which):
+            for half in range(HALVES):
                 for a in which:
                     one_pass(sums[t, half][side], a, t, half)
 
-        sums = {}
-        for half in range(HALVES):
-            open_sums(sums, 0, half)
-            passes(cloth_pass, 0, sums, 0, half, (0,))
-            passes(trim_pass, 1, sums, 0, half, (0,))
+        for t in range(2):
+            open_sums(t)
+            passes(cloth_pass, 0, t, (0,))
+            passes(trim_pass, 1, t, (0,))
         gather_v(1, v_tab1)
         v2_tab = held([P, T3], I32, "v2_tab", "v_scale_tab")
         nc.sync.dma_start(v2_tab[:], tab2_words[0].rearrange("p t i -> p (t i)").bitcast(I32))
         quantize_w1_last(w1_last)
-        for half in range(HALVES):
-            passes(cloth_pass, 0, sums, 0, half, (1,))
-        for half in range(HALVES):
-            passes(trim_pass, 1, sums, 0, half, (1,))
-        trim_out = held([P, 2 * HALVES, BANK], F32, "trim_out", "w1_grouped0")
-        summed = [combine(sums, 0, half, trim_out) for half in range(HALVES)]
-        for half in range(HALVES):
-            apply_gain(summed[half], 0, half)
-        for half in range(HALVES):
-            open_sums(sums, 1, half)
-            passes(cloth_pass, 0, sums, 1, half, (0, 1))
-            passes(trim_pass, 1, sums, 1, half, (0, 1))
-            apply_gain(combine(sums, 1, half), 1, half)
+        v2_scale = held([P, S2], U8, "v2_scale", "w4_raw")
+        nc.gpsimd.memset(v2_scale[:].bitcast(I32), 0)
+        for r in range(4):
+            nc.sync.dma_start(
+                v2_scale[r:P:32, :].bitcast(I32), v2_scale_picked[4 + r : 20 : 4, :].bitcast(I32)
+            )
+        for t in range(2):
+            passes(cloth_pass, 0, t, (1,))
+        for t in range(2):
+            passes(trim_pass, 1, t, (1,))
+        trim_out = held([P, GPSIMD_SUMS, BANK], F32, "trim_out", "w4_scale_raw")
+        for t in range(2):
+            combine(t)
+        for t in range(2, PACK):
+            open_sums(t)
+            passes(cloth_pass, 0, t, (0, 1))
+            passes(trim_pass, 1, t, (0, 1))
+            combine(t)
+        for t in range(PACK):
+            apply_gain(t)
         v2_codes = held([P, S2], U32, "v2_codes")
         nc.vector.tensor_copy(out=v2_codes[:], in_=v2_tab[:].bitcast(U32).indirect(offs2_t[:]))
 

@@ -25,7 +25,9 @@ HALVES = S // BANK
 M_TILES = S2 // P
 NH = N // 2
 LIST_ROWS = 16
-GPSIMD_SUMS = 5
+QUADRANTS = (0, 2, 1, 3)
+SCALAR_SHARE = 48
+GPSIMD_SUMS = 4
 
 
 def tile_list_garment_decade_scores_kernel(
@@ -36,10 +38,13 @@ def tile_list_garment_decade_scores_kernel(
     with ExitStack() as ctx:
         keep = ctx.enter_context(tc.tile_pool(name="keep", bufs=1))
         ring = ctx.enter_context(tc.tile_pool(name="ring", bufs=6))
-        psum = ctx.enter_context(tc.psum_pool(name="psum", bufs=8))
+        psum = ctx.enter_context(tc.psum_pool(name="psum", bufs=1))
 
         def held(shape, dtype, name, tag=None):
             return keep.tile(shape, dtype, name=name, tag=tag or name, align_bytes=64)
+
+        def bank(shape, number):
+            return psum.tile(shape, F32, name="bank%d" % number)
 
         w4_scale_raw = held([P, PASSES * H], U8, "w4_scale_raw")
         v2_scale_tab = held([P, T3], U8, "v2_scale_tab")
@@ -76,10 +81,10 @@ def tile_list_garment_decade_scores_kernel(
         w1_raw0 = held([P, PACK, H], F32, "w1_raw0")
         nc.sync.dma_start(w1_raw0[:], w1[0:512, :].rearrange("(p i) c -> p i c", i=PACK))
         nc.sync.dma_start(offs2_t[:], offs2)
-        for r in range(4):
+        for q in QUADRANTS:
             nc.sync.dma_start(
-                w4_scale_raw[r:P:32, :].bitcast(I32).rearrange("q (a c) -> q a c", a=PASSES),
-                w4_scales.rearrange("a (q r) c -> r q a c", r=4)[r].bitcast(I32),
+                w4_scale_raw[32 * q : 32 * q + 4, :].bitcast(I32).rearrange("r (a c) -> r a c", a=PASSES),
+                w4_scales[:, 4 * q : 4 * q + 4, :].rearrange("a r c -> r a c").bitcast(I32),
             )
         v_tab0 = held([P, T], I32, "v_tab0")
         load_v(v_tab0, 0, 0)
@@ -90,11 +95,11 @@ def tile_list_garment_decade_scores_kernel(
         nc.vector.tensor_copy(out=v_scale_picked[:], in_=v_scale_tab[:].indirect(offs_t[:]))
 
         def move_v_scale(a):
-            for r in range(4):
-                row = 96 + 16 * a
+            for q in QUADRANTS:
+                row = 96 + 16 * a + 4 * q
                 nc.sync.dma_start(
-                    v_scale[r:P:32, S * a : S * (a + 1)].bitcast(I32),
-                    v_scale_picked[row + r : row + 16 : 4, :].bitcast(I32),
+                    v_scale[32 * q : 32 * q + 4, S * a : S * (a + 1)].bitcast(I32),
+                    v_scale_picked[row : row + 4, :].bitcast(I32),
                 )
 
         w4_codes = held([P, PASSES * H * 2], U8, "w4_codes")
@@ -106,22 +111,21 @@ def tile_list_garment_decade_scores_kernel(
         w1_codes = [held([P, H], U32, "w1_codes%d" % a) for a in range(PASSES)]
         w1_scale = [held([P, H], U8, "w1_scale%d" % a) for a in range(PASSES)]
 
-        def regroup_w1(copy, grouped, raw, first, count, offset):
+        def regroup_w1(copy, grouped, raw, first, last):
             copy(
-                out=grouped[:].rearrange("p (t m i) -> p m i t", t=PACK, i=PACK)[:, first : first + count],
-                in_=raw[:].rearrange("p i (m t) -> p m i t", t=PACK)[:, first - offset : first - offset + count],
+                out=grouped[:].rearrange("p (t m i) -> p m i t", t=PACK, i=PACK)[:, first:last],
+                in_=raw[:].rearrange("p i (m t) -> p m i t", t=PACK)[:, first:last],
             )
 
         def quantize_w1_first(raw):
             grouped = held([P, PACK * H], BF16, "w1_grouped0")
-            regroup_w1(nc.scalar.copy, grouped, raw, 0, P, 0)
+            regroup_w1(nc.scalar.copy, grouped, raw, 0, P)
             nc.vector.quantize_mx(out=w1_codes[0][:].bitcast(FP8X4), scales=w1_scale[0][:], in_=grouped[:])
 
-        def quantize_w1_last(parts):
+        def quantize_w1_last(raw):
             grouped = held([P, PACK * H], BF16, "w1_grouped1")
-            regroup_w1(nc.scalar.copy, grouped, parts[0], 0, 64, 0)
-            regroup_w1(nc.scalar.copy, grouped, parts[1], 64, 32, 64)
-            regroup_w1(nc.vector.tensor_copy, grouped, parts[1], 96, 32, 64)
+            regroup_w1(nc.scalar.copy, grouped, raw, 0, SCALAR_SHARE)
+            regroup_w1(nc.vector.tensor_copy, grouped, raw, SCALAR_SHARE, P)
             for first, last in ((0, P), (P, 2 * P), (2 * P, H)):
                 nc.vector.quantize_mx(
                     out=w1_codes[1][:, first:last].bitcast(FP8X4), scales=w1_scale[1][:, first:last],
@@ -154,13 +158,8 @@ def tile_list_garment_decade_scores_kernel(
         move_v_scale(0)
         load_v(v_tab1, 1, 1)
         move_v_scale(1)
-        w1_last = []
-        for part, tag in enumerate(("w4_raw", "w4_scale_raw")):
-            w1_last.append(held([P, PACK, H // 2], F32, "w1_last%d" % part, tag))
-            nc.sync.dma_start(
-                w1_last[part][:],
-                w1[512:1024, H // 2 * part : H // 2 * (part + 1)].rearrange("(p i) c -> p i c", i=PACK),
-            )
+        w1_raw1 = held([P, PACK, H], F32, "w1_raw1", "w4_raw")
+        nc.sync.dma_start(w1_raw1[:], w1[512:1024, :].rearrange("(p i) c -> p i c", i=PACK))
 
         shade_rows = shade.rearrange("(p t) j -> p t j", t=PACK)
         shade_t = []
@@ -171,7 +170,7 @@ def tile_list_garment_decade_scores_kernel(
         nc.sync.dma_start(pos1_t[:], pos1)
         nc.sync.dma_start(pos2_t[:], pos2)
 
-        turned = psum.tile([P, P], F32, name="bank")
+        turned = bank([P, P], 7)
         nc.tensor.transpose(turned[:], row_consts[:], identity[:])
         col_consts = held([P, 2 * M_TILES], F32, "col_consts")
         nc.scalar.copy(out=col_consts[:], in_=turned[:, 0 : 2 * M_TILES])
@@ -206,74 +205,78 @@ def tile_list_garment_decade_scores_kernel(
 
         summed = [held([P, PACK, BANK], F32, "summed%d" % half) for half in range(HALVES)]
 
+        cloth, trim = {}, {}
+
+        def cloth_passes(t, half, which):
+            if 0 in which:
+                cloth[t, half] = bank([P, BANK], HALVES * t + half)
+            for a in which:
+                cloth_pass(cloth[t, half], a, t, half)
+
+        def trim_passes(t, half, which):
+            if 0 in which:
+                trim[t, half] = bank([P, BANK], (HALVES * t + half + 4) % 8)
+            for a in which:
+                trim_pass(trim[t, half], a, t, half)
+
         def combine(t):
             shaded = [ring.tile([P, BANK], F32, name="shaded") for half in range(HALVES)]
             for half in range(HALVES):
                 nc.vector.tensor_tensor(
-                    out=shaded[half][:], in0=sums[t, half][0][:],
-                    in1=shade_t[t][:, BANK * half : BANK * (half + 1)], op=ALU.mult,
+                    out=shaded[half][:], in0=shade_t[t][:, BANK * half : BANK * (half + 1)],
+                    in1=cloth[t, half][:], op=ALU.mult,
                 )
             for half in range(HALVES):
-                trim = sums[t, half][1]
                 place = HALVES * t + half
                 if place < GPSIMD_SUMS:
-                    nc.scalar.copy(out=trim_out[:, place, :], in_=trim[:])
                     nc.gpsimd.tensor_tensor(
                         out=summed[half][:, t, :], in0=trim_out[:, place, :], in1=shaded[half][:], op=ALU.add
                     )
                 else:
-                    nc.vector.tensor_tensor(out=summed[half][:, t, :], in0=trim[:], in1=shaded[half][:], op=ALU.add)
+                    nc.vector.tensor_tensor(
+                        out=summed[half][:, t, :], in0=shaded[half][:], in1=trim[t, half][:], op=ALU.add
+                    )
 
-        def apply_gain(t):
-            for half in range(HALVES):
-                nc.scalar.activation(
-                    out=h[t][:, BANK * half : BANK * (half + 1)], in_=summed[half][:, t, :], func=ACT.Copy,
-                    scale=gain_t[:, t : t + 1],
-                )
-
-        sums = {}
-
-        def open_sums(t):
-            for half in range(HALVES):
-                sums[t, half] = (
-                    psum.tile([P, BANK], F32, name="bank"),
-                    psum.tile([P, BANK], F32, name="bank"),
-                )
-
-        def passes(one_pass, side, t, which):
-            for half in range(HALVES):
-                for a in which:
-                    one_pass(sums[t, half][side], a, t, half)
-
-        for t in range(2):
-            open_sums(t)
-            passes(cloth_pass, 0, t, (0,))
-            passes(trim_pass, 1, t, (0,))
+        pieces = [(t, half) for t in range(PACK) for half in range(HALVES)]
+        early = pieces[:4]
+        for t, half in early:
+            cloth_passes(t, half, (0,))
+        for t, half in early:
+            trim_passes(t, half, (0,))
         gather_v(1, v_tab1)
         v2_tab = held([P, T3], I32, "v2_tab", "v_scale_tab")
         nc.sync.dma_start(v2_tab[:], tab2_words[0].rearrange("p t i -> p (t i)").bitcast(I32))
-        quantize_w1_last(w1_last)
-        v2_scale = held([P, S2], U8, "v2_scale", "w4_raw")
+        quantize_w1_last(w1_raw1)
+        v2_scale = held([P, S2], U8, "v2_scale", "w1_grouped1")
         nc.gpsimd.memset(v2_scale[:].bitcast(I32), 0)
-        for r in range(4):
+        for q in QUADRANTS:
             nc.sync.dma_start(
-                v2_scale[r:P:32, :].bitcast(I32), v2_scale_picked[4 + r : 20 : 4, :].bitcast(I32)
+                v2_scale[32 * q : 32 * q + 4, :].bitcast(I32), v2_scale_picked[4 + 4 * q : 8 + 4 * q, :].bitcast(I32)
             )
-        for t in range(2):
-            passes(cloth_pass, 0, t, (1,))
-        for t in range(2):
-            passes(trim_pass, 1, t, (1,))
-        trim_out = held([P, GPSIMD_SUMS, BANK], F32, "trim_out", "w4_scale_raw")
-        for t in range(2):
-            combine(t)
-        for t in range(2, PACK):
-            open_sums(t)
-            passes(cloth_pass, 0, t, (0, 1))
-            passes(trim_pass, 1, t, (0, 1))
-            combine(t)
+        for t, half in early:
+            cloth_passes(t, half, (1,))
+        for half in range(HALVES):
+            for t in range(2):
+                trim_passes(t, half, (1,))
+        trim_out = held([P, GPSIMD_SUMS, BANK], F32, "trim_out", "w4_raw")
+        for place, (t, half) in enumerate(pieces[:GPSIMD_SUMS]):
+            if (t, half) not in early:
+                trim_passes(t, half, (0, 1))
+            nc.scalar.copy(out=trim_out[:, place, :], in_=trim[t, half][:])
         for t in range(PACK):
-            apply_gain(t)
-        v2_codes = held([P, S2], U32, "v2_codes")
+            for half in range(HALVES):
+                if (t, half) not in early:
+                    cloth_passes(t, half, (0, 1))
+            for half in range(HALVES):
+                if (t, half) not in pieces[:GPSIMD_SUMS]:
+                    trim_passes(t, half, (0, 1))
+            combine(t)
+        for t, half in pieces:
+            nc.scalar.activation(
+                out=h[t][:, BANK * half : BANK * (half + 1)], in_=summed[half][:, t, :], func=ACT.Copy,
+                scale=gain_t[:, t : t + 1],
+            )
+        v2_codes = held([P, S2], U32, "v2_codes", "w4_raw")
         nc.vector.tensor_copy(out=v2_codes[:], in_=v2_tab[:].bitcast(U32).indirect(offs2_t[:]))
 
         def pick(name, tag, offsets, width):
@@ -310,7 +313,7 @@ def tile_list_garment_decade_scores_kernel(
             )
 
         cols = NH // LIST_ROWS
-        picked1 = pick("picked1", None, pos1_t[:], N)
+        picked1 = pick("picked1", "summed0", pos1_t[:], N)
         grouped1 = interleave("grouped1", "reused", picked1, ACT.Abs, N)
         picked2a = pick("picked2a", "summed1", pos2_t[:, 0:cols], NH)
         x1 = quantize("x1", grouped1, N)
@@ -325,7 +328,7 @@ def tile_list_garment_decade_scores_kernel(
 
         def seam_scores(tiles):
             for i in tiles:
-                acc = psum.tile([P, BANK], F32, name="bank")
+                acc = bank([P, BANK], i)
                 scores(acc[:], i, x1)
                 nc.scalar.activation(out=seam[i][:], in_=acc[:], func=ACT.Copy, scale=col_consts[:, i : i + 1])
 
@@ -341,8 +344,8 @@ def tile_list_garment_decade_scores_kernel(
                 in1=seam[i][:, cols], op0=ALU.max, op1=ALU.add,
             )
 
-        def half_scores(x2, pair):
-            acc = psum.tile([P, 2, NH], F32, name="bank")
+        def half_scores(x2, half, pair):
+            acc = bank([P, 2, NH], 2 * half + pair)
             for u in range(2):
                 scores(acc[:, u, :], 2 * pair + u, x2)
             return acc
@@ -356,14 +359,24 @@ def tile_list_garment_decade_scores_kernel(
             nc.sync.dma_start(out_rows[:, 2 * pair : 2 * pair + 2, cols], result[:])
             return made
 
-        finish_half(half_scores(x2a, 0), 0, 0)
-        x2b = finish_half(half_scores(x2a, 1), 0, 1, lambda: quantize("x2b", grouped2b, NH))
+        finish_half(half_scores(x2a, 0, 0), 0, 0)
+        x2b = finish_half(half_scores(x2a, 0, 1), 0, 1, lambda: quantize("x2b", grouped2b, NH))
         for pair in range(2):
-            finish_half(half_scores(x2b, pair), 1, pair)
-        for i in range(4, M_TILES):
-            acc = psum.tile([P, 2, NH], F32, name="bank")
+            finish_half(half_scores(x2b, 1, pair), 1, pair)
+
+        def whole_scores(i):
+            acc = bank([P, 2, NH], i - 4)
             scores(acc[:, 0, :], i, x2a)
             scores(acc[:, 1, :], i, x2b)
+            return acc
+
+        for i in range(4, M_TILES - 1):
             result = held([P, N], F32, "result%d" % i)
-            finish(result[:], acc[:].rearrange("p u n -> p (u n)"), i, slice(0, N))
+            finish(result[:], whole_scores(i)[:].rearrange("p u n -> p (u n)"), i, slice(0, N))
             nc.sync.dma_start(out_rows[:, i, :], result[:])
+        acc = whole_scores(M_TILES - 1)
+        for half in range(2):
+            cols = slice(NH * half, NH * (half + 1))
+            result = held([P, NH], F32, "result_last%d" % half)
+            finish(result[:], acc[:, half, :], M_TILES - 1, cols)
+            nc.sync.dma_start(out_rows[:, M_TILES - 1, cols], result[:])

from contextlib import ExitStack

import concourse.mybir as mybir
from concourse.masks import make_identity

K, H, T, S, T3, S2, N = 1024, 512, 4096, 1024, 2048, 1024, 512
FLOPS = 2 * (2 * K * H * S) + 2 * (2 * H * S2 * N)

F32 = mybir.dt.float32
BF16 = mybir.dt.bfloat16
I32 = mybir.dt.int32
U32 = mybir.dt.uint32
U16 = mybir.dt.uint16
U8 = mybir.dt.uint8
FP8X4 = mybir.dt.float8_e4m3fn_x4
FP4X4 = mybir.dt.float4_e2m1fn_x4
ALU = mybir.AluOpType
ACT = mybir.ActivationFunctionType

P = 128
PACK = 4
PASSES = K // (P * PACK)
BANK = 512
HALVES = S // BANK
M_TILES = S2 // P
NH = N // 2
LIST_ROWS = 16
QUADRANTS = (0, 2, 1, 3)
SCALAR_SHARE = 48
GPSIMD_SUMS = 4


def tile_list_garment_decade_scores_kernel(
    tc, tab_words, tab_scales, tab2_words, tab2_scales, offs, offs2, pos1, pos2,
    w1, w4_words, w4_scales, shade, gain, seamw, level, out,
):
    nc = tc.nc
    with ExitStack() as ctx:
        keep = ctx.enter_context(tc.tile_pool(name="keep", bufs=1))
        ring = ctx.enter_context(tc.tile_pool(name="ring", bufs=6))
        psum = ctx.enter_context(tc.psum_pool(name="psum", bufs=1))

        def held(shape, dtype, name, tag=None):
            return keep.tile(shape, dtype, name=name, tag=tag or name, align_bytes=64)

        def bank(shape, number):
            return psum.tile(shape, F32, name="bank%d" % number)

        w4_scale_raw = held([P, PASSES * H], U8, "w4_scale_raw")
        v2_scale_tab = held([P, T3], U8, "v2_scale_tab")
        v_scale_tab = held([P, T], U8, "v_scale_tab")
        nc.vector.memset(w4_scale_raw[:].bitcast(I32), 0)
        nc.vector.memset(v2_scale_tab[:].bitcast(I32), 0)
        nc.vector.memset(v_scale_tab[0:96, :].bitcast(I32), 0)
        v_scale = held([P, PASSES * S], U8, "v_scale")
        nc.gpsimd.memset(v_scale[:].bitcast(I32), 0)

        identity = held([P, P], F32, "identity")
        row_consts = held([P, P], F32, "row_consts")
        nc.gpsimd.memset(row_consts[:], 0.0)
        nc.gpsimd.dma_start(row_consts[0:M_TILES, :], seamw.rearrange("(i p) -> i p", p=P))
        nc.gpsimd.dma_start(row_consts[M_TILES : 2 * M_TILES, :], level.rearrange("(i p) -> i p", p=P))
        make_identity(nc, identity[:])

        offs_t = held([P, S // LIST_ROWS], U16, "offs_t")
        offs2_t = held([P, S2 // LIST_ROWS], U16, "offs2_t")
        pos1_t = held([P, N // LIST_ROWS], U16, "pos1_t")
        pos2_t = held([P, N // LIST_ROWS], U16, "pos2_t")
        w4_raw = held([P, PASSES, H // 2], I32, "w4_raw")
        gain_t = held([P, PACK], F32, "gain_t")

        def load_v(tile, a, part):
            cols = slice(T // 2 * part, T // 2 * (part + 1))
            nc.sync.dma_start(tile[:, cols], tab_words[a].rearrange("p t i -> p (t i)").bitcast(I32)[:, cols])

        nc.sync.dma_start(offs_t[:], offs)
        nc.sync.dma_start(
            v_scale_tab[96:P, :].bitcast(I32), tab_scales.rearrange("a q t -> (a q) t").bitcast(I32)
        )
        nc.sync.dma_start(w4_raw[:], w4_words.rearrange("a p c -> p a c").bitcast(I32))
        w1_raw0 = held([P, PACK, H], F32, "w1_raw0")
        nc.sync.dma_start(w1_raw0[:], w1[0:512, :].rearrange("(p i) c -> p i c", i=PACK))
        nc.sync.dma_start(offs2_t[:], offs2)
        for q in QUADRANTS:
            nc.sync.dma_start(
                w4_scale_raw[32 * q : 32 * q + 4, :].bitcast(I32).rearrange("r (a c) -> r a c", a=PASSES),
                w4_scales[:, 4 * q : 4 * q + 4, :].rearrange("a r c -> r a c").bitcast(I32),
            )
        v_tab0 = held([P, T], I32, "v_tab0")
        load_v(v_tab0, 0, 0)
        nc.sync.dma_start(v2_scale_tab[4:20, :].bitcast(I32), tab2_scales[0].bitcast(I32))
        load_v(v_tab0, 0, 1)

        v_scale_picked = held([P, S], U8, "v_scale_picked")
        nc.vector.tensor_copy(out=v_scale_picked[:], in_=v_scale_tab[:].indirect(offs_t[:]))

        def move_v_scale(a):
            for q in QUADRANTS:
                row = 96 + 16 * a + 4 * q
                nc.sync.dma_start(
                    v_scale[32 * q : 32 * q + 4, S * a : S * (a + 1)].bitcast(I32),
                    v_scale_picked[row : row + 4, :].bitcast(I32),
                )

        w4_codes = held([P, PASSES * H * 2], U8, "w4_codes")
        nc.vector.tensor_copy(
            out=w4_codes[:].bitcast(U16).rearrange("p (a t m) -> p a t m", a=PASSES, t=PACK),
            in_=w4_raw[:].rearrange("p a c -> p (a c)").bitcast(U16).rearrange("p (a m t) -> p a t m", a=PASSES, t=PACK),
        )

        w1_codes = [held([P, H], U32, "w1_codes%d" % a) for a in range(PASSES)]
        w1_scale = [held([P, H], U8, "w1_scale%d" % a) for a in range(PASSES)]

        def regroup_w1(copy, grouped, raw, first, last):
            copy(
                out=grouped[:].rearrange("p (t m i) -> p m i t", t=PACK, i=PACK)[:, first:last],
                in_=raw[:].rearrange("p i (m t) -> p m i t", t=PACK)[:, first:last],
            )

        def quantize_w1_first(raw):
            grouped = held([P, PACK * H], BF16, "w1_grouped0")
            regroup_w1(nc.scalar.copy, grouped, raw, 0, P)
            nc.vector.quantize_mx(out=w1_codes[0][:].bitcast(FP8X4), scales=w1_scale[0][:], in_=grouped[:])

        def quantize_w1_last(raw):
            grouped = held([P, PACK * H], BF16, "w1_grouped1")
            regroup_w1(nc.scalar.copy, grouped, raw, 0, SCALAR_SHARE)
            regroup_w1(nc.vector.tensor_copy, grouped, raw, SCALAR_SHARE, P)
            for first, last in ((0, P), (P, 2 * P), (2 * P, H)):
                nc.vector.quantize_mx(
                    out=w1_codes[1][:, first:last].bitcast(FP8X4), scales=w1_scale[1][:, first:last],
                    in_=grouped[:, PACK * first : PACK * last],
                )

        v_codes = {}

        def gather_v(a, tile):
            for half in range(HALVES):
                v_codes[a, half] = held([P, BANK], U32, "v_codes%d%d" % (a, half))
                cols = BANK // LIST_ROWS
                nc.vector.tensor_copy(
                    out=v_codes[a, half][:],
                    in_=tile[:].bitcast(U32).indirect(offs_t[:, cols * half : cols * (half + 1)]),
                )

        quantize_w1_first(w1_raw0)
        w4_scale = held([P, PASSES * H], U8, "w4_scale")
        nc.vector.tensor_copy(
            out=w4_scale[:].rearrange("p (a t m) -> p a t m", a=PASSES, t=PACK),
            in_=w4_scale_raw[:].rearrange("p (a m t) -> p a t m", a=PASSES, t=PACK),
        )
        v2_scale_picked = held([P, S2], U8, "v2_scale_picked")
        nc.vector.tensor_copy(out=v2_scale_picked[:], in_=v2_scale_tab[:].indirect(offs2_t[:]))
        gather_v(0, v_tab0)

        v_tab1 = held([P, T], I32, "v_tab1", "v_scale_tab")
        load_v(v_tab1, 1, 0)
        move_v_scale(0)
        load_v(v_tab1, 1, 1)
        move_v_scale(1)
        w1_raw1 = held([P, PACK, H], F32, "w1_raw1", "w4_raw")
        nc.sync.dma_start(w1_raw1[:], w1[512:1024, :].rearrange("(p i) c -> p i c", i=PACK))

        shade_rows = shade.rearrange("(p t) j -> p t j", t=PACK)
        shade_t = []
        for t, tag in enumerate(("w1_raw0", "w1_grouped0", "v_tab0", "v_scale_picked")):
            shade_t.append(held([P, S], F32, "shade%d" % t, tag))
            nc.sync.dma_start(shade_t[t][:], shade_rows[:, t, :])
        nc.sync.dma_start(gain_t[:], gain.rearrange("(p t) -> p t", t=PACK))
        nc.sync.dma_start(pos1_t[:], pos1)
        nc.sync.dma_start(pos2_t[:], pos2)

        turned = bank([P, P], 7)
        nc.tensor.transpose(turned[:], row_consts[:], identity[:])
        col_consts = held([P, 2 * M_TILES], F32, "col_consts")
        nc.scalar.copy(out=col_consts[:], in_=turned[:, 0 : 2 * M_TILES])

        def cloth_pass(acc, a, t, half):
            cols = slice(S * a + BANK * half, S * a + BANK * (half + 1))
            rows = slice(P * t, P * (t + 1))
            nc.tensor.matmul_mx(
                out=acc[:],
                lhsT=w1_codes[a][:, rows].bitcast(FP8X4),
                lhsT_scale=w1_scale[a][:, rows],
                rhs=v_codes[a, half][:].bitcast(FP8X4),
                rhs_scale=v_scale[:, cols],
                start=(a == 0),
                stop=(a == PASSES - 1),
            )

        def trim_pass(acc, a, t, half):
            cols = slice(S * a + BANK * half, S * a + BANK * (half + 1))
            first = H * a + P * t
            nc.tensor.matmul_mx(
                out=acc[:],
                lhsT=w4_codes[:, 2 * first : 2 * (first + P)].bitcast(FP4X4),
                lhsT_scale=w4_scale[:, first : first + P],
                rhs=v_codes[a, half][:].bitcast(FP8X4),
                rhs_scale=v_scale[:, cols],
                start=(a == 0),
                stop=(a == PASSES - 1),
            )

        h = [held([P, S], F32, "h%d" % t) for t in range(PACK)]

        summed = [held([P, PACK, BANK], F32, "summed%d" % half) for half in range(HALVES)]

        cloth, trim = {}, {}

        def cloth_passes(t, half, which):
            if 0 in which:
                cloth[t, half] = bank([P, BANK], HALVES * t + half)
            for a in which:
                cloth_pass(cloth[t, half], a, t, half)

        def trim_passes(t, half, which):
            if 0 in which:
                trim[t, half] = bank([P, BANK], (HALVES * t + half + 4) % 8)
            for a in which:
                trim_pass(trim[t, half], a, t, half)

        def combine(t):
            shaded = [ring.tile([P, BANK], F32, name="shaded") for half in range(HALVES)]
            for half in range(HALVES):
                nc.vector.tensor_tensor(
                    out=shaded[half][:], in0=shade_t[t][:, BANK * half : BANK * (half + 1)],
                    in1=cloth[t, half][:], op=ALU.mult,
                )
            for half in range(HALVES):
                place = HALVES * t + half
                if place < GPSIMD_SUMS:
                    nc.gpsimd.tensor_tensor(
                        out=summed[half][:, t, :], in0=trim_out[:, place, :], in1=shaded[half][:], op=ALU.add
                    )
                else:
                    nc.vector.tensor_tensor(
                        out=summed[half][:, t, :], in0=shaded[half][:], in1=trim[t, half][:], op=ALU.add
                    )

        pieces = [(t, half) for t in range(PACK) for half in range(HALVES)]
        early = pieces[:4]
        for t, half in early:
            cloth_passes(t, half, (0,))
        for t, half in early:
            trim_passes(t, half, (0,))
        gather_v(1, v_tab1)
        v2_tab = held([P, T3], I32, "v2_tab", "v_scale_tab")
        nc.sync.dma_start(v2_tab[:], tab2_words[0].rearrange("p t i -> p (t i)").bitcast(I32))
        quantize_w1_last(w1_raw1)
        v2_scale = held([P, S2], U8, "v2_scale", "w1_grouped1")
        nc.gpsimd.memset(v2_scale[:].bitcast(I32), 0)
        for q in QUADRANTS:
            nc.sync.dma_start(
                v2_scale[32 * q : 32 * q + 4, :].bitcast(I32), v2_scale_picked[4 + 4 * q : 8 + 4 * q, :].bitcast(I32)
            )
        for t, half in early:
            cloth_passes(t, half, (1,))
        for half in range(HALVES):
            for t in range(2):
                trim_passes(t, half, (1,))
        trim_out = held([P, GPSIMD_SUMS, BANK], F32, "trim_out", "w4_raw")
        for place, (t, half) in enumerate(pieces[:GPSIMD_SUMS]):
            if (t, half) not in early:
                trim_passes(t, half, (0, 1))
            nc.scalar.copy(out=trim_out[:, place, :], in_=trim[t, half][:])
        for t in range(PACK):
            for half in range(HALVES):
                if (t, half) not in early:
                    cloth_passes(t, half, (0, 1))
            for half in range(HALVES):
                if (t, half) not in pieces[:GPSIMD_SUMS]:
                    trim_passes(t, half, (0, 1))
            combine(t)
        for t, half in pieces:
            nc.scalar.activation(
                out=h[t][:, BANK * half : BANK * (half + 1)], in_=summed[half][:, t, :], func=ACT.Copy,
                scale=gain_t[:, t : t + 1],
            )
        v2_codes = held([P, S2], U32, "v2_codes", "w4_raw")
        nc.vector.tensor_copy(out=v2_codes[:], in_=v2_tab[:].bitcast(U32).indirect(offs2_t[:]))

        def pick(name, tag, offsets, width):
            picked = held([P, PACK, width], F32, name, tag)
            for t in range(PACK):
                nc.vector.tensor_copy(out=picked[:, t, :], in_=h[t][:].indirect(offsets))
            return picked

        def interleave(name, tag, picked, func, width):
            grouped = held([P, PACK * width], BF16, name, tag)
            nc.scalar.activation(
                out=grouped[:].rearrange("p (c i t) -> p c t i", i=4, t=PACK),
                in_=picked[:].rearrange("p t (c i) -> p c t i", i=4),
                func=func,
            )
            return grouped

        def quantize(name, grouped, width):
            codes = held([P, width], U32, name + "_codes")
            scale = held([P, width], U8, name + "_scale")
            nc.vector.quantize_mx(out=codes[:].bitcast(FP8X4), scales=scale[:], in_=grouped[:])
            return codes, scale

        def scores(acc, i, x):
            rows = slice(P * i, P * (i + 1))
            nc.tensor.matmul_mx(
                out=acc,
                lhsT=v2_codes[:, rows].bitcast(FP8X4),
                lhsT_scale=v2_scale[:, rows],
                rhs=x[0][:].bitcast(FP8X4),
                rhs_scale=x[1][:],
                start=True,
                stop=True,
            )

        cols = NH // LIST_ROWS
        picked1 = pick("picked1", "summed0", pos1_t[:], N)
        grouped1 = interleave("grouped1", "reused", picked1, ACT.Abs, N)
        picked2a = pick("picked2a", "summed1", pos2_t[:, 0:cols], NH)
        x1 = quantize("x1", grouped1, N)
        grouped2a = interleave("grouped2a", None, picked2a, ACT.Copy, NH)
        picked2b = held([P, PACK, NH], F32, "picked2b", "reused")
        for t in range(PACK):
            nc.vector.tensor_copy(out=picked2b[:, t, :], in_=h[t][:].indirect(pos2_t[:, cols : 2 * cols]))
            if t == 1:
                x2a = quantize("x2a", grouped2a, NH)

        seam = [held([P, N], F32, "seam%d" % i) for i in range(M_TILES)]

        def seam_scores(tiles):
            for i in tiles:
                acc = bank([P, BANK], i)
                scores(acc[:], i, x1)
                nc.scalar.activation(out=seam[i][:], in_=acc[:], func=ACT.Copy, scale=col_consts[:, i : i + 1])

        seam_scores(range(0, 4))
        grouped2b = interleave("grouped2b", None, picked2b, ACT.Copy, NH)
        seam_scores(range(4, 8))

        out_rows = out.rearrange("(i p) n -> p i n", p=P)

        def finish(result, acc, i, cols):
            nc.vector.scalar_tensor_tensor(
                out=result, in0=acc, scalar=col_consts[:, M_TILES + i : M_TILES + i + 1],
                in1=seam[i][:, cols], op0=ALU.max, op1=ALU.add,
            )

        def half_scores(x2, half, pair):
            acc = bank([P, 2, NH], 2 * half + pair)
            for u in range(2):
                scores(acc[:, u, :], 2 * pair + u, x2)
            return acc

        def finish_half(acc, half, pair, between=None):
            cols = slice(NH * half, NH * (half + 1))
            result = held([P, 2, NH], F32, "result%d%d" % (half, pair))
            finish(result[:, 0, :], acc[:, 0, :], 2 * pair, cols)
            made = between() if between else None
            finish(result[:, 1, :], acc[:, 1, :], 2 * pair + 1, cols)
            nc.sync.dma_start(out_rows[:, 2 * pair : 2 * pair + 2, cols], result[:])
            return made

        finish_half(half_scores(x2a, 0, 0), 0, 0)
        x2b = finish_half(half_scores(x2a, 0, 1), 0, 1, lambda: quantize("x2b", grouped2b, NH))
        for pair in range(2):
            finish_half(half_scores(x2b, 1, pair), 1, pair)

        def whole_scores(i):
            acc = bank([P, 2, NH], i - 4)
            scores(acc[:, 0, :], i, x2a)
            scores(acc[:, 1, :], i, x2b)
            return acc

        for i in range(4, M_TILES - 1):
            result = held([P, N], F32, "result%d" % i)
            finish(result[:], whole_scores(i)[:].rearrange("p u n -> p (u n)"), i, slice(0, N))
            nc.sync.dma_start(out_rows[:, i, :], result[:])
        acc = whole_scores(M_TILES - 1)
        for half in range(2):
            cols = slice(NH * half, NH * (half + 1))
            result = held([P, NH], F32, "result_last%d" % half)
            finish(result[:], acc[:, half, :], M_TILES - 1, cols)
            nc.sync.dma_start(out_rows[:, M_TILES - 1, cols], result[:])
